import numpy as np, ml_dtypes
CORES = [8,11,14,16,19,22,24,27,30]
N = 9
TOK, K, FT = 32, 2, 4
ROUTE = [[[3,6],[4,6],[4,5],[1,3],[4,6],[0,2],[4,7],[5,7],[1,5],[5,8],[1,6],[4,8],[2,3],[6,7],[0,4],[2,7],[2,7],[1,6],[1,3],[3,8],[0,6],[0,1],[7,8],[5,6],[5,6],[3,6],[5,8],[0,5],[0,4],[1,8],[1,3],[3,5]],[[2,5],[4,7],[5,7],[5,8],[5,8],[4,8],[2,7],[7,8],[3,5],[3,4],[2,8],[5,8],[0,7],[2,8],[3,5],[5,8],[0,3],[4,6],[6,8],[5,8],[5,7],[2,8],[1,6],[2,3],[6,8],[1,4],[6,8],[3,6],[7,8],[1,2],[3,8],[6,8]],[[4,5],[4,8],[0,5],[1,4],[5,6],[2,3],[4,6],[0,5],[5,8],[3,6],[3,8],[4,7],[1,6],[4,5],[3,6],[1,8],[0,3],[2,4],[6,8],[2,4],[5,7],[0,8],[1,3],[0,5],[0,4],[1,5],[5,7],[5,7],[0,5],[3,4],[6,7],[1,8]],[[1,8],[0,2],[6,7],[2,3],[4,5],[4,5],[1,5],[5,7],[2,6],[0,3],[1,7],[2,6],[2,3],[6,8],[1,8],[2,6],[5,7],[4,7],[3,6],[2,3],[7,8],[3,7],[1,3],[5,8],[6,7],[2,7],[4,6],[4,5],[0,5],[3,5],[5,8],[4,5]],[[6,8],[4,5],[5,7],[2,7],[3,7],[3,5],[1,4],[0,4],[3,5],[1,3],[1,6],[1,7],[4,8],[4,8],[5,6],[5,7],[1,4],[2,7],[5,7],[6,7],[0,1],[0,3],[3,5],[5,7],[5,6],[3,6],[0,3],[2,8],[0,5],[6,7],[4,8],[7,8]],[[2,7],[1,8],[5,8],[7,8],[1,3],[6,7],[1,6],[1,5],[3,7],[0,5],[1,7],[2,3],[3,4],[2,5],[6,7],[0,3],[0,5],[3,7],[1,5],[0,5],[6,8],[4,5],[6,7],[2,3],[3,5],[0,3],[4,8],[4,6],[0,3],[6,8],[6,7],[2,3]],[[0,7],[0,6],[1,7],[5,6],[0,3],[2,3],[2,3],[2,5],[1,8],[3,8],[4,7],[1,2],[3,8],[0,5],[1,7],[2,3],[1,3],[5,8],[4,7],[0,8],[1,6],[5,8],[5,8],[7,8],[0,2],[1,2],[2,7],[1,8],[0,8],[0,1],[4,6],[3,4]],[[2,8],[3,8],[3,5],[2,3],[4,7],[4,7],[0,3],[0,8],[2,3],[3,6],[3,7],[1,6],[0,3],[4,8],[5,6],[0,4],[0,1],[4,7],[1,6],[2,7],[2,6],[1,5],[3,8],[1,2],[0,7],[0,4],[2,5],[0,1],[3,4],[1,8],[6,8],[0,7]],[[0,8],[3,5],[3,7],[1,5],[1,4],[4,8],[1,7],[1,4],[2,5],[0,6],[2,8],[0,4],[2,3],[2,4],[5,7],[2,6],[1,5],[2,8],[1,2],[3,4],[3,5],[4,7],[0,2],[2,4],[2,4],[0,4],[1,7],[2,5],[3,4],[5,6],[5,6],[1,4]]]
def setup_inputs(rng):
    return {"x": rng.standard_normal((N, 128, TOK), dtype=np.float32).astype(ml_dtypes.bfloat16), "gate": (0.5 * rng.integers(1, 4, size=(N, K, TOK)) * (2 * rng.integers(0, 2, size=(N, K, TOK)) - 1)).astype(np.float32).astype(ml_dtypes.bfloat16), "w1": (rng.standard_normal((N, 128, FT * 128), dtype=np.float32) / 8).astype(ml_dtypes.bfloat16), "w2": (rng.standard_normal((N, 128, FT * 128), dtype=np.float32) / 8).astype(ml_dtypes.bfloat16)}
def setup_inputs_big(rng):
    d = setup_inputs(rng)
    for k in ("x", "gate", "w1", "w2"): d[k] = (d[k].astype(np.float32) * 1024.0).astype(d[k].dtype)
    return d
def setup_inputs_small(rng):
    d = setup_inputs(rng)
    for k in ("x", "gate", "w1", "w2"): d[k] = (d[k].astype(np.float32) * (1 / 1024.0)).astype(d[k].dtype)
    return d
def reference(x, gate, w1, w2):
    X, GATE, W1, W2 = x.astype(np.float64), gate.astype(np.float64), w1.astype(np.float64), w2.astype(np.float64)
    y = np.zeros((N, 128, TOK))
    for r in range(N):
        for t in range(TOK):
            for i, e in enumerate(ROUTE[r][t]):
                hid = np.maximum(W1[e].T @ X[r][:, t], 0.0)
                y[r][:, t] += GATE[r][i, t] * sum(W2[e][:, 128 * f:128 * f + 128].T @ hid[128 * f:128 * f + 128] for f in range(FT))
    return {"y": y.astype(ml_dtypes.bfloat16)}

@@ -1,0 +1,285 @@
+from concourse.bass import DstId, RemoteDMATransfer
+from concourse.mybir import AluOpType
+
+_N, _TOK, _FT, _GS = 9, 32, 4, 3
+_GW = _GS * _TOK
+_NG = _N // _GS
+
+SCRATCH = {
+    "xall": ("sbuf", [128, _N * _TOK], "bfloat16"),
+    "w1s": ("sbuf", [128, _FT * 128], "bfloat16"),
+    "w2s": ("sbuf", [128, _FT * 128], "bfloat16"),
+    "zer": ("sbuf", [128, _FT * _GW], "bfloat16"),
+    "zz": ("sbuf", [128, 2 * _GW], "bfloat16"),
+    "qq": ("sbuf", [128, _GW], "bfloat16"),
+    "land": ("sbuf", [128, _N * _TOK], "bfloat16"),
+    "grow": ("sbuf", [128, 2 * _TOK], "bfloat16"),
+    "ones": ("sbuf", [128, 128], "bfloat16"),
+    "prod": ("sbuf", [128, _N * _TOK], "float32"),
+    "tmp": ("sbuf", [128, 3 * _NG * _TOK], "float32"),
+    "ybf": ("sbuf", [128, _TOK], "bfloat16"),
+    "pg": ("psum", [128, 512], "float32"),
+    "pm": ("psum", [128, 512], "float32"),
+}
+for _k in range(_NG):
+    SCRATCH["h%d" % _k] = ("sbuf", [128, _FT * _GW], "bfloat16")
+    SCRATCH["ro%d" % _k] = ("sbuf", [128, _GW], "bfloat16")
+    SCRATCH["pa%d" % _k] = ("psum", [128, 512], "float32")
+    SCRATCH["pr%d" % _k] = ("psum", [128, 512], "float32")
+
+SEMAPHORES = ["sx", "sg", "sw1", "sw2", "sone", "sgb", "sv", "sz", "sq", "syr", "sy", "sloc"]
+for _k in range(_NG):
+    SEMAPHORES += ["sxg%d" % _k, "sa%d" % _k, "sh%d" % _k, "sr%d" % _k, "sc%d" % _k, "sl%d" % _k]
+
+
+def _bits(mask):
+    return [i for i in range(16) if (mask >> i) & 1]
+
+
+def _m(engs):
+    out = 0
+    for e in engs:
+        out |= 1 << e
+    return out
+
+
+def _plan(T, topo):
+    cores = list(T.cores)
+    n = len(cores)
+    chips = []
+    for c in cores:
+        if topo.chip(c) not in chips:
+            chips.append(topo.chip(c))
+    groups = [[r for r in range(n) if topo.chip(cores[r]) == ch] for ch in chips]
+    gi = [chips.index(topo.chip(c)) for c in cores]
+    ng = len(groups)
+    assert [r for grp in groups for r in grp] == list(range(n)) and all(len(grp) == _GS for grp in groups)
+
+    def ok(a, k):
+        return all(topo.may_write(cores[a], cores[r]) for r in groups[k] if r != a)
+
+    def links(ka, kb):
+        return 1 if (topo.mates(chips[ka], chips[kb]) or topo.same_plane(chips[ka], chips[kb])) else 2
+
+    eng = []
+    for a in range(n):
+        m = 0xFFFF
+        for b in range(n):
+            if a != b:
+                m &= topo.mask(cores[a], cores[b])
+        eng.append(_bits(m)[:8])
+        assert len(eng[a]) == 8
+
+    needy = [sorted([k for k in range(ng) if k != gi[e] and not ok(e, k)], key=lambda k: links(gi[e], k))
+             for e in range(n)]
+    job = [None] * n
+    via = {}
+    for e in range(n):
+        for k in needy[e]:
+            p = [p for p in groups[gi[e]] if p != e and ok(p, k) and job[p] is None][0]
+            job[p] = (e, k)
+            via[(e, k)] = p
+
+    order = []
+    for e in range(n):
+        rem = sorted([k for k in range(ng) if k != gi[e]], key=lambda k: links(gi[e], k))
+        if needy[e]:
+            rem = needy[e] + [k for k in rem if k not in needy[e]]
+        elif job[e] is not None:
+            rem = [k for k in rem if k != job[e][1]] + [job[e][1]]
+        order.append([gi[e]] + rem)
+
+    hop2 = [[] for _ in range(n)]
+    for k in range(ng):
+        dests = [d for d in range(n) if gi[d] != k]
+        elig = {d: [s for s in groups[k] if topo.may_write(cores[s], cores[d])] for d in dests}
+        for d in sorted(dests, key=lambda d: len(elig[d])):
+            s = min(elig[d], key=lambda s: len(hop2[s]))
+            hop2[s].append(d)
+    for s in range(n):
+        hop2[s].sort(key=lambda d: (order[d].index(gi[s]), 0 if needy[d] else 1))
+
+    lcol = [[None] * n for _ in range(n)]
+    for r in range(n):
+        for k in range(ng):
+            seq = []
+            for p in groups[k]:
+                if k != gi[r] and gi[r] in needy[p]:
+                    continue
+                seq.append(p)
+                if k != gi[r] and job[p] is not None and job[p][1] == gi[r]:
+                    seq.append(job[p][0])
+            for j, e in enumerate(seq):
+                lcol[r][e] = k * _GW + j * _TOK
+
+    calls = [[] for _ in range(n)]
+    expect = [[0] * ng for _ in range(n)]
+    for e in range(n):
+        E = eng[e]
+        pats = [[E[0:4], E[4:6], E[6:8]], [E[4:8], E[0:2], E[2:4]]]
+        for idx, k in enumerate(order[e]):
+            tr = []
+            if idx == 0:
+                peers = [r for r in groups[k] if r != e]
+                for r, en in zip(peers, [E[0:4], E[4:8]]):
+                    tr.append((r, "ro%d" % k, groups[k].index(r) * _TOK, _TOK, "land", lcol[r][e], "sl%d" % gi[e], en))
+                calls[e].append(("sc%d" % k, 1, tr))
+            elif k in needy[e]:
+                tr.append((via[(e, k)], "ro%d" % k, 0, _GW, "qq", 0, "sq", E))
+                calls[e].append(("sc%d" % k, 1, tr))
+            elif job[e] is not None and job[e][1] == k:
+                for j, (r, en) in enumerate(zip(groups[k], pats[idx - 1])):
+                    tr.append((r, "zz", j * 2 * _TOK, 2 * _TOK, "land", lcol[r][e], "sl%d" % gi[e], en))
+                calls[e].append(("sz", 2 * _GS, tr))
+            else:
+                for j, (r, en) in enumerate(zip(groups[k], pats[idx - 1])):
+                    tr.append((r, "ro%d" % k, j * _TOK, _TOK, "land", lcol[r][e], "sl%d" % gi[e], en))
+                calls[e].append(("sc%d" % k, 1, tr))
+            for t in tr:
+                if t[4] == "land":
+                    expect[t[0]][gi[e]] += len(t[7])
+
+    corder = []
+    for r in range(n):
+        rem = [k for k in range(ng) if k != gi[r]]
+        rem.sort(key=lambda k: (1 if any(gi[r] in needy[p] for p in groups[k]) else 0, links(k, gi[r])))
+        corder.append([gi[r]] + rem)
+    return dict(cores=cores, groups=groups, gi=gi, eng=eng, needy=needy, job=job, order=order, hop2=hop2,
+                lcol=lcol, calls=calls, expect=expect, corder=corder)
+
+
+def rank_program(g, core, T, topo):
+    me = T.rank_of(core)
+    if me is None:
+        return
+    P = _plan(T, topo)
+    S = T.sem
+    cores, groups, gi = P["cores"], P["groups"], P["gi"]
+    route = T.tables["ROUTE"]
+    k0 = gi[me]
+    E = P["eng"][me]
+    v, tq = g.vector, g.tensor
+    own = me * _TOK
+    loc = [0]
+
+    def dst_id(r):
+        rid, pid, _se = topo.addr(cores[r])
+        return DstId(rid=rid, pnc=pid)
+
+    g.sync.dma_start(T.xall[:, own:own + _TOK], T.x[:, :]).then_inc(S.sx, 16)
+    g.scalar.dma_start(T.grow[0:1, 0:2 * _TOK], T.gate[:, :]).then_inc(S.sg, 16)
+    g.scalar.dma_start(T.w1s[:, :], T.w1[:, :]).then_inc(S.sw1, 16)
+    g.sync.dma_start(T.w2s[:, :], T.w2[:, :]).then_inc(S.sw2, 16)
+
+    g.wait_ge(S.sx, 16)
+    peers = [r for r in groups[k0] if r != me]
+    blk = T.xall[:, own:own + _TOK]
+    g.remote_dma_fused([RemoteDMATransfer(dst_ids=[dst_id(r) for r in peers], dma_engine_mask=_m(E),
+                                          remote_sem=S["sxg%d" % k0], srcs=[blk], dsts=[blk for _ in peers])],
+                       local_sem=S.sloc)
+    loc[0] += len(E)
+    if P["hop2"][me]:
+        g.wait_ge(S["sxg%d" % k0], len(E) * len(peers))
+        cb = T.xall[:, k0 * _GW:(k0 + 1) * _GW]
+        g.remote_dma_fused([RemoteDMATransfer(dst_ids=[dst_id(d) for d in P["hop2"][me]], dma_engine_mask=_m(E),
+                                              remote_sem=S["sxg%d" % k0], srcs=[cb], dsts=[cb for _ in P["hop2"][me]])],
+                           local_sem=S.sloc)
+        loc[0] += len(E)
+    for sem, cnt, tr in P["calls"][me]:
+        g.wait_ge(S[sem], cnt)
+        g.remote_dma_fused([RemoteDMATransfer(dst_ids=[dst_id(r)], dma_engine_mask=_m(en), remote_sem=S[rs],
+                                              src=T[sb][:, sc:sc + w], dst=T[db][:, dc:dc + w])
+                            for (r, sb, sc, w, db, dc, rs, en) in tr], local_sem=S.sloc)
+        loc[0] += sum(len(t[7]) for t in tr)
+    g.wait_ge(S.sloc, loc[0])
+
+    tq.wait_ge(S.sone, 1)
+    tq.wait_ge(S.sg, 16)
+    tq.matmul(T.pg[:, 0:2 * _TOK], T.ones[0:1, :], T.grow[0:1, 0:2 * _TOK], True, True).then_inc(S.sgb, 1)
+    for idx, k in enumerate(P["order"][me]):
+        if idx == 0:
+            tq.wait_ge(S.sx, 16)
+            tq.wait_ge(S.sw1, 16)
+            tq.wait_ge(S["sxg%d" % k], len(E) * len(peers))
+        else:
+            tq.wait_ge(S["sxg%d" % k], len(E))
+        for f in range(_FT):
+            tq.matmul(T["pa%d" % k][:, f * _GW:(f + 1) * _GW], T.w1s[:, f * 128:(f + 1) * 128],
+                      T.xall[:, k * _GW:(k + 1) * _GW], True, True).then_inc(S["sa%d" % k], 1)
+        if idx == 0:
+            tq.wait_ge(S.sw2, 16)
+        tq.wait_ge(S["sh%d" % k], 1)
+        for f in range(_FT):
+            tq.matmul(T["pr%d" % k][:, 0:_GW], T.w2s[:, f * 128:(f + 1) * 128],
+                      T["h%d" % k][:, f * _GW:(f + 1) * _GW], f == 0, f == _FT - 1).then_inc(S["sr%d" % k], 1)
+
+    vc = [0]
+
+    def vop(inst):
+        inst.then_inc(S.sv, 1)
+        vc[0] += 1
+
+    def vsync():
+        v.wait_ge(S.sv, vc[0])
+
+    v.memset(T.ones[0:1, :], 1.0).then_inc(S.sone, 1)
+    vop(v.memset(T.zer[:, :], 0.0))
+    vop(v.memset(T.pm[:, 0:_N * _TOK], 0.0))
+    v.wait_ge(S.sgb, 1)
+    vsync()
+    for i in range(len(route[me][0])):
+        t = 0
+        while t < _TOK:
+            e = route[me][t][i]
+            u = t + 1
+            while u < _TOK and route[me][u][i] == e:
+                u += 1
+            c = P["lcol"][me][e]
+            vop(v.tensor_copy(T.pm[:, c + t:c + u], T.pg[:, i * _TOK + t:i * _TOK + u]))
+            t = u
+    job = P["job"][me]
+    for idx, k in enumerate(P["order"][me]):
+        v.wait_ge(S["sa%d" % k], _FT)
+        v.tensor_tensor(T["h%d" % k][:, :], T["pa%d" % k][:, 0:_FT * _GW], T.zer[:, :], AluOpType.max).then_inc(S["sh%d" % k], 1)
+        v.wait_ge(S["sr%d" % k], _FT)
+        if job is not None and job[1] == k:
+            for j in range(_GS):
+                v.tensor_copy(T.zz[:, 2 * j * _TOK:(2 * j + 1) * _TOK],
+                              T["pr%d" % k][:, j * _TOK:(j + 1) * _TOK]).then_inc(S.sz, 1)
+        else:
+            v.tensor_copy(T["ro%d" % k][:, :], T["pr%d" % k][:, 0:_GW]).then_inc(S["sc%d" % k], 1)
+        if idx == 0:
+            j = groups[k].index(me)
+            c = P["lcol"][me][me]
+            vop(v.tensor_copy(T.land[:, c:c + _TOK], T["pr%d" % k][:, j * _TOK:(j + 1) * _TOK]))
+    if job is not None:
+        v.wait_ge(S.sq, len(E))
+        for j in range(_GS):
+            v.tensor_copy(T.zz[:, (2 * j + 1) * _TOK:(2 * j + 2) * _TOK],
+                          T.qq[:, j * _TOK:(j + 1) * _TOK]).then_inc(S.sz, 1)
+    acc = None
+    co = P["corder"][me]
+    for idx, k in enumerate(co):
+        v.wait_ge(S["sl%d" % k], P["expect"][me][k])
+        vsync()
+        a, b = k * _GW, (k + 1) * _GW
+        vop(v.tensor_tensor(T.prod[:, a:b], T.land[:, a:b], T.pm[:, a:b], AluOpType.mult))
+        vsync()
+        t0 = T.tmp[:, (3 * idx) * _TOK:(3 * idx + 1) * _TOK]
+        t1 = T.tmp[:, (3 * idx + 1) * _TOK:(3 * idx + 2) * _TOK]
+        t2 = T.tmp[:, (3 * idx + 2) * _TOK:(3 * idx + 3) * _TOK]
+        vop(v.tensor_tensor(t0, T.prod[:, a:a + _TOK], T.prod[:, a + _TOK:a + 2 * _TOK], AluOpType.add))
+        third = T.prod[:, a + 2 * _TOK:b]
+        if acc is not None:
+            vop(v.tensor_tensor(t1, third, acc, AluOpType.add))
+            third = t1
+        vsync()
+        if idx == len(co) - 1:
+            v.tensor_tensor(T.ybf[:, :], t0, third, AluOpType.add).then_inc(S.syr, 1)
+        else:
+            vop(v.tensor_tensor(t2, t0, third, AluOpType.add))
+            acc = t2
+
+    g.sync.wait_ge(S.syr, 1)
+    g.sync.dma_start(T.y[:, :], T.ybf[:, :]).then_inc(S.sy, 16)
+    g.sync.wait_ge(S.sy, 16)

@@ -4,32 +4,36 @@ from concourse.mybir import AluOpType
 _N, _TOK, _FT, _GS = 9, 32, 4, 3
 _GW = _GS * _TOK
 _NG = _N // _GS
+_NE = 8
+_LG = _GW + _TOK
+_HT = _FT // 2
 
 SCRATCH = {
     "xall": ("sbuf", [128, _N * _TOK], "bfloat16"),
     "w1s": ("sbuf", [128, _FT * 128], "bfloat16"),
     "w2s": ("sbuf", [128, _FT * 128], "bfloat16"),
     "zer": ("sbuf", [128, _FT * _GW], "bfloat16"),
-    "zz": ("sbuf", [128, 2 * _GW], "bfloat16"),
-    "qq": ("sbuf", [128, _GW], "bfloat16"),
-    "land": ("sbuf", [128, _N * _TOK], "bfloat16"),
+    "zz": ("sbuf", [128, 5 * _TOK], "bfloat16"),
+    "land": ("sbuf", [128, _NG * _LG], "bfloat16"),
     "grow": ("sbuf", [128, 2 * _TOK], "bfloat16"),
     "ones": ("sbuf", [128, 128], "bfloat16"),
-    "prod": ("sbuf", [128, _N * _TOK], "float32"),
+    "prod": ("sbuf", [128, _NG * _LG], "float32"),
     "tmp": ("sbuf", [128, 3 * _NG * _TOK], "float32"),
     "ybf": ("sbuf", [128, _TOK], "bfloat16"),
-    "pg": ("psum", [128, 512], "float32"),
     "pm": ("psum", [128, 512], "float32"),
+    "pa00": ("psum", [128, 512], "float32"),
+    "pa01": ("psum", [128, 512], "float32"),
+    "pa10": ("psum", [128, 512], "float32"),
+    "pa11": ("psum", [128, 512], "float32"),
 }
 for _k in range(_NG):
     SCRATCH["h%d" % _k] = ("sbuf", [128, _FT * _GW], "bfloat16")
     SCRATCH["ro%d" % _k] = ("sbuf", [128, _GW], "bfloat16")
-    SCRATCH["pa%d" % _k] = ("psum", [128, 512], "float32")
     SCRATCH["pr%d" % _k] = ("psum", [128, 512], "float32")
 
-SEMAPHORES = ["sx", "sg", "sw1", "sw2", "sone", "sgb", "sv", "sz", "sq", "syr", "sy", "sloc"]
+SEMAPHORES = ["sx", "sg", "sw1", "sw2", "sone", "spm", "sgm", "sv", "sz", "sq", "syr", "sy", "sloc"]
 for _k in range(_NG):
-    SEMAPHORES += ["sxg%d" % _k, "sa%d" % _k, "sh%d" % _k, "sr%d" % _k, "sc%d" % _k, "sl%d" % _k]
+    SEMAPHORES += ["sxg%d" % _k, "saa%d" % _k, "sab%d" % _k, "sha%d" % _k, "shb%d" % _k, "sr%d" % _k, "sc%d" % _k, "sl%d" % _k]
 
 
 def _bits(mask):
@@ -67,8 +71,8 @@ def _plan(T, topo):
         for b in range(n):
             if a != b:
                 m &= topo.mask(cores[a], cores[b])
-        eng.append(_bits(m)[:8])
-        assert len(eng[a]) == 8
+        eng.append(_bits(m)[:_NE])
+        assert len(eng[a]) == _NE
 
     needy = [sorted([k for k in range(ng) if k != gi[e] and not ok(e, k)], key=lambda k: links(gi[e], k))
              for e in range(n)]
@@ -102,49 +106,58 @@ def _plan(T, topo):
     lcol = [[None] * n for _ in range(n)]
     for r in range(n):
         for k in range(ng):
-            seq = []
-            for p in groups[k]:
-                if k != gi[r] and gi[r] in needy[p]:
-                    continue
-                seq.append(p)
-                if k != gi[r] and job[p] is not None and job[p][1] == gi[r]:
-                    seq.append(job[p][0])
-            for j, e in enumerate(seq):
-                lcol[r][e] = k * _GW + j * _TOK
+            B = k * _LG + _TOK
+            nd = [e for e in groups[k] if gi[r] in needy[e]]
+            if not nd:
+                for j, e in enumerate(groups[k]):
+                    lcol[r][e] = B + j * _TOK
+            else:
+                e = nd[0]
+                p = via[(e, gi[r])]
+                o = [x for x in groups[k] if x != e and x != p][0]
+                first = groups[gi[r]].index(r) == 0
+                lcol[r][p] = B if first else B + _TOK
+                lcol[r][e] = B + _TOK if first else B
+                lcol[r][o] = B + 2 * _TOK
 
     calls = [[] for _ in range(n)]
     expect = [[0] * ng for _ in range(n)]
     for e in range(n):
         E = eng[e]
-        pats = [[E[0:4], E[4:6], E[6:8]], [E[4:8], E[0:2], E[2:4]]]
+        hf, qt = len(E) // 2, len(E) // 4
+        pats = [[E[0:hf], E[hf:hf + qt], E[hf + qt:]], [E[hf:], E[0:qt], E[qt:hf]]]
+        sl = "sl%d" % gi[e]
         for idx, k in enumerate(order[e]):
-            tr = []
             if idx == 0:
                 peers = [r for r in groups[k] if r != e]
-                for r, en in zip(peers, [E[0:4], E[4:8]]):
-                    tr.append((r, "ro%d" % k, groups[k].index(r) * _TOK, _TOK, "land", lcol[r][e], "sl%d" % gi[e], en))
-                calls[e].append(("sc%d" % k, 1, tr))
+                new = [([("sc%d" % k, 1)], [(r, "ro%d" % k, groups[k].index(r) * _TOK, _TOK, "land", lcol[r][e], sl, en)
+                                            for r, en in zip(peers, [E[0:hf], E[hf:]])])]
             elif k in needy[e]:
-                tr.append((via[(e, k)], "ro%d" % k, 0, _GW, "qq", 0, "sq", E))
-                calls[e].append(("sc%d" % k, 1, tr))
+                new = [([("sc%d" % k, 1)], [(via[(e, k)], "ro%d" % k, 0, _GW, "zz", _TOK, "sq", E)])]
             elif job[e] is not None and job[e][1] == k:
-                for j, (r, en) in enumerate(zip(groups[k], pats[idx - 1])):
-                    tr.append((r, "zz", j * 2 * _TOK, 2 * _TOK, "land", lcol[r][e], "sl%d" % gi[e], en))
-                calls[e].append(("sz", 2 * _GS, tr))
+                ha, hb, hc = groups[k]
+                pt = pats[idx - 1]
+                new = [([("sc%d" % k, 1)], [(hb, "ro%d" % k, _TOK, _TOK, "land", lcol[hb][e], sl, E)]),
+                       ([("sz", 2), ("sq", len(eng[job[e][0]]))],
+                        [(ha, "zz", 0, 2 * _TOK, "land", lcol[ha][e], sl, pt[0]),
+                         (hb, "zz", _TOK, 2 * _TOK, "land", lcol[hb][job[e][0]] - _TOK, sl, pt[1]),
+                         (hc, "zz", 3 * _TOK, 2 * _TOK, "land", lcol[hc][job[e][0]], sl, pt[2])])]
             else:
-                for j, (r, en) in enumerate(zip(groups[k], pats[idx - 1])):
-                    tr.append((r, "ro%d" % k, j * _TOK, _TOK, "land", lcol[r][e], "sl%d" % gi[e], en))
-                calls[e].append(("sc%d" % k, 1, tr))
-            for t in tr:
-                if t[4] == "land":
-                    expect[t[0]][gi[e]] += len(t[7])
+                new = [([("sc%d" % k, 1)], [(r, "ro%d" % k, j * _TOK, _TOK, "land", lcol[r][e], sl, en)
+                                            for j, (r, en) in enumerate(zip(groups[k], pats[idx - 1]))])]
+            calls[e] += new
+            for _w, tr in new:
+                for t in tr:
+                    if t[4] == "land":
+                        expect[t[0]][gi[e]] += len(t[7])
 
     corder = []
     for r in range(n):
         rem = [k for k in range(ng) if k != gi[r]]
         rem.sort(key=lambda k: (1 if any(gi[r] in needy[p] for p in groups[k]) else 0, links(k, gi[r])))
         corder.append([gi[r]] + rem)
-    return dict(cores=cores, groups=groups, gi=gi, eng=eng, needy=needy, job=job, order=order, hop2=hop2,
+    ilv = [len(needy[e]) == ng - 1 for e in range(n)]
+    return dict(cores=cores, groups=groups, gi=gi, eng=eng, ilv=ilv, needy=needy, job=job, order=order, hop2=hop2,
                 lcol=lcol, calls=calls, expect=expect, corder=corder)
 
 
@@ -158,6 +171,8 @@ def rank_program(g, core, T, topo):
     route = T.tables["ROUTE"]
     k0 = gi[me]
     E = P["eng"][me]
+    order = P["order"][me]
+    co = P["corder"][me]
     v, tq = g.vector, g.tensor
     own = me * _TOK
     loc = [0]
@@ -185,18 +200,37 @@ def rank_program(g, core, T, topo):
                                               remote_sem=S["sxg%d" % k0], srcs=[cb], dsts=[cb for _ in P["hop2"][me]])],
                            local_sem=S.sloc)
         loc[0] += len(E)
-    for sem, cnt, tr in P["calls"][me]:
-        g.wait_ge(S[sem], cnt)
+    for waits, tr in P["calls"][me]:
+        for sem, cnt in waits:
+            g.wait_ge(S[sem], cnt)
         g.remote_dma_fused([RemoteDMATransfer(dst_ids=[dst_id(r)], dma_engine_mask=_m(en), remote_sem=S[rs],
                                               src=T[sb][:, sc:sc + w], dst=T[db][:, dc:dc + w])
                             for (r, sb, sc, w, db, dc, rs, en) in tr], local_sem=S.sloc)
         loc[0] += sum(len(t[7]) for t in tr)
     g.wait_ge(S.sloc, loc[0])
 
-    tq.wait_ge(S.sone, 1)
-    tq.wait_ge(S.sg, 16)
-    tq.matmul(T.pg[:, 0:2 * _TOK], T.ones[0:1, :], T.grow[0:1, 0:2 * _TOK], True, True).then_inc(S.sgb, 1)
-    for idx, k in enumerate(P["order"][me]):
+    runs = {k: [] for k in co}
+    for i in range(len(route[me][0])):
+        t = 0
+        while t < _TOK:
+            e = route[me][t][i]
+            u = t + 1
+            while u < _TOK and route[me][u][i] == e:
+                u += 1
+            runs[gi[e]].append((i * _TOK + t, P["lcol"][me][e] + t, u - t))
+            t = u
+    ngm = sum(len(r) for r in runs.values())
+
+    def gm(k):
+        for (gc, lc, ln) in runs[k]:
+            tq.matmul(T.pm[:, lc:lc + ln], T.ones[0:1, :], T.grow[0:1, gc:gc + ln], True, True).then_inc(S.sgm, 1)
+
+    def pa(idx, hf):
+        return T["pa%d%d" % (idx % 2, hf)]
+
+    HW = _HT * _GW
+
+    def mm1(idx, k):
         if idx == 0:
             tq.wait_ge(S.sx, 16)
             tq.wait_ge(S.sw1, 16)
@@ -204,14 +238,37 @@ def rank_program(g, core, T, topo):
         else:
             tq.wait_ge(S["sxg%d" % k], len(E))
         for f in range(_FT):
-            tq.matmul(T["pa%d" % k][:, f * _GW:(f + 1) * _GW], T.w1s[:, f * 128:(f + 1) * 128],
-                      T.xall[:, k * _GW:(k + 1) * _GW], True, True).then_inc(S["sa%d" % k], 1)
+            hf, q = f // _HT, f % _HT
+            tq.matmul(pa(idx, hf)[:, q * _GW:(q + 1) * _GW], T.w1s[:, f * 128:(f + 1) * 128],
+                      T.xall[:, k * _GW:(k + 1) * _GW], True, True).then_inc(S[("sab%d" if hf else "saa%d") % k], 1)
+
+    def mm2(idx, k):
         if idx == 0:
             tq.wait_ge(S.sw2, 16)
-        tq.wait_ge(S["sh%d" % k], 1)
         for f in range(_FT):
+            if f % _HT == 0:
+                tq.wait_ge(S[("shb%d" if f // _HT else "sha%d") % k], 1)
             tq.matmul(T["pr%d" % k][:, 0:_GW], T.w2s[:, f * 128:(f + 1) * 128],
                       T["h%d" % k][:, f * _GW:(f + 1) * _GW], f == 0, f == _FT - 1).then_inc(S["sr%d" % k], 1)
+
+    tq.wait_ge(S.sone, 1)
+    tq.wait_ge(S.sg, 16)
+    tq.wait_ge(S.spm, 1)
+    gm(co[0])
+    gm(co[1])
+    mm1(0, order[0])
+    mm2(0, order[0])
+    if P["ilv"][me]:
+        mm1(1, order[1])
+        mm1(2, order[2])
+        mm2(1, order[1])
+        mm2(2, order[2])
+    else:
+        mm1(1, order[1])
+        mm2(1, order[1])
+        mm1(2, order[2])
+        mm2(2, order[2])
+    gm(co[2])
 
     vc = [0]
 
@@ -223,46 +280,49 @@ def rank_program(g, core, T, topo):
         v.wait_ge(S.sv, vc[0])
 
     v.memset(T.ones[0:1, :], 1.0).then_inc(S.sone, 1)
-    vop(v.memset(T.zer[:, :], 0.0))
-    vop(v.memset(T.pm[:, 0:_N * _TOK], 0.0))
-    v.wait_ge(S.sgb, 1)
+    v.memset(T.pm[:, 0:_NG * _LG], 0.0).then_inc(S.spm, 1)
+    vop(v.memset(T.zer[:, 0:HW], 0.0))
     vsync()
-    for i in range(len(route[me][0])):
-        t = 0
-        while t < _TOK:
-            e = route[me][t][i]
-            u = t + 1
-            while u < _TOK and route[me][u][i] == e:
-                u += 1
-            c = P["lcol"][me][e]
-            vop(v.tensor_copy(T.pm[:, c + t:c + u], T.pg[:, i * _TOK + t:i * _TOK + u]))
-            t = u
     job = P["job"][me]
-    for idx, k in enumerate(P["order"][me]):
-        v.wait_ge(S["sa%d" % k], _FT)
-        v.tensor_tensor(T["h%d" % k][:, :], T["pa%d" % k][:, 0:_FT * _GW], T.zer[:, :], AluOpType.max).then_inc(S["sh%d" % k], 1)
+
+    def relu(idx, k):
+        for hf in range(2):
+            v.wait_ge(S[("sab%d" if hf else "saa%d") % k], _HT)
+            v.tensor_tensor(T["h%d" % k][:, hf * HW:(hf + 1) * HW], pa(idx, hf)[:, 0:HW], T.zer[:, 0:HW],
+                            AluOpType.max).then_inc(S[("shb%d" if hf else "sha%d") % k], 1)
+
+    def out(idx, k):
         v.wait_ge(S["sr%d" % k], _FT)
         if job is not None and job[1] == k:
-            for j in range(_GS):
-                v.tensor_copy(T.zz[:, 2 * j * _TOK:(2 * j + 1) * _TOK],
-                              T["pr%d" % k][:, j * _TOK:(j + 1) * _TOK]).then_inc(S.sz, 1)
+            pr = T["pr%d" % k]
+            v.tensor_copy(T["ro%d" % k][:, _TOK:2 * _TOK], pr[:, _TOK:2 * _TOK]).then_inc(S["sc%d" % k], 1)
+            v.tensor_copy(T.zz[:, 0:_TOK], pr[:, 0:_TOK]).then_inc(S.sz, 1)
+            v.tensor_copy(T.zz[:, 4 * _TOK:5 * _TOK], pr[:, 2 * _TOK:3 * _TOK]).then_inc(S.sz, 1)
         else:
             v.tensor_copy(T["ro%d" % k][:, :], T["pr%d" % k][:, 0:_GW]).then_inc(S["sc%d" % k], 1)
         if idx == 0:
             j = groups[k].index(me)
             c = P["lcol"][me][me]
             vop(v.tensor_copy(T.land[:, c:c + _TOK], T["pr%d" % k][:, j * _TOK:(j + 1) * _TOK]))
-    if job is not None:
-        v.wait_ge(S.sq, len(E))
-        for j in range(_GS):
-            v.tensor_copy(T.zz[:, (2 * j + 1) * _TOK:(2 * j + 2) * _TOK],
-                          T.qq[:, j * _TOK:(j + 1) * _TOK]).then_inc(S.sz, 1)
+
+    relu(0, order[0])
+    out(0, order[0])
+    if P["ilv"][me]:
+        relu(1, order[1])
+        relu(2, order[2])
+        out(1, order[1])
+        out(2, order[2])
+    else:
+        relu(1, order[1])
+        out(1, order[1])
+        relu(2, order[2])
+        out(2, order[2])
+    v.wait_ge(S.sgm, ngm)
     acc = None
-    co = P["corder"][me]
     for idx, k in enumerate(co):
         v.wait_ge(S["sl%d" % k], P["expect"][me][k])
         vsync()
-        a, b = k * _GW, (k + 1) * _GW
+        a, b = k * _LG + _TOK, (k + 1) * _LG
         vop(v.tensor_tensor(T.prod[:, a:b], T.land[:, a:b], T.pm[:, a:b], AluOpType.mult))
         vsync()
         t0 = T.tmp[:, (3 * idx) * _TOK:(3 * idx + 1) * _TOK]

from concourse.bass import DstId, RemoteDMATransfer
from concourse.mybir import AluOpType

_N, _TOK, _FT, _GS = 9, 32, 4, 3
_GW = _GS * _TOK
_NG = _N // _GS
_NE = 8
_LG = _GW + _TOK
_HT = _FT // 2

SCRATCH = {
    "xall": ("sbuf", [128, _N * _TOK], "bfloat16"),
    "w1s": ("sbuf", [128, _FT * 128], "bfloat16"),
    "w2s": ("sbuf", [128, _FT * 128], "bfloat16"),
    "zer": ("sbuf", [128, _FT * _GW], "bfloat16"),
    "zz": ("sbuf", [128, 5 * _TOK], "bfloat16"),
    "land": ("sbuf", [128, _NG * _LG], "bfloat16"),
    "grow": ("sbuf", [128, 2 * _TOK], "bfloat16"),
    "ones": ("sbuf", [128, 128], "bfloat16"),
    "prod": ("sbuf", [128, _NG * _LG], "float32"),
    "tmp": ("sbuf", [128, 3 * _NG * _TOK], "float32"),
    "ybf": ("sbuf", [128, _TOK], "bfloat16"),
    "pm": ("psum", [128, 512], "float32"),
    "pa00": ("psum", [128, 512], "float32"),
    "pa01": ("psum", [128, 512], "float32"),
    "pa10": ("psum", [128, 512], "float32"),
    "pa11": ("psum", [128, 512], "float32"),
}
for _k in range(_NG):
    SCRATCH["h%d" % _k] = ("sbuf", [128, _FT * _GW], "bfloat16")
    SCRATCH["ro%d" % _k] = ("sbuf", [128, _GW], "bfloat16")
    SCRATCH["pr%d" % _k] = ("psum", [128, 512], "float32")

SEMAPHORES = ["sx", "sg", "sw1", "sw2", "sone", "spm", "sgm", "sv", "sz", "sq", "syr", "sy", "sloc"]
for _k in range(_NG):
    SEMAPHORES += ["sxg%d" % _k, "saa%d" % _k, "sab%d" % _k, "sha%d" % _k, "shb%d" % _k, "sr%d" % _k, "sc%d" % _k, "sl%d" % _k]


def _bits(mask):
    return [i for i in range(16) if (mask >> i) & 1]


def _m(engs):
    out = 0
    for e in engs:
        out |= 1 << e
    return out


def _plan(T, topo):
    cores = list(T.cores)
    n = len(cores)
    chips = []
    for c in cores:
        if topo.chip(c) not in chips:
            chips.append(topo.chip(c))
    groups = [[r for r in range(n) if topo.chip(cores[r]) == ch] for ch in chips]
    gi = [chips.index(topo.chip(c)) for c in cores]
    ng = len(groups)
    assert [r for grp in groups for r in grp] == list(range(n)) and all(len(grp) == _GS for grp in groups)

    def ok(a, k):
        return all(topo.may_write(cores[a], cores[r]) for r in groups[k] if r != a)

    def links(ka, kb):
        return 1 if (topo.mates(chips[ka], chips[kb]) or topo.same_plane(chips[ka], chips[kb])) else 2

    eng = []
    for a in range(n):
        m = 0xFFFF
        for b in range(n):
            if a != b:
                m &= topo.mask(cores[a], cores[b])
        eng.append(_bits(m)[:_NE])
        assert len(eng[a]) == _NE

    needy = [sorted([k for k in range(ng) if k != gi[e] and not ok(e, k)], key=lambda k: links(gi[e], k))
             for e in range(n)]
    job = [None] * n
    via = {}
    for e in range(n):
        for k in needy[e]:
            p = [p for p in groups[gi[e]] if p != e and ok(p, k) and job[p] is None][0]
            job[p] = (e, k)
            via[(e, k)] = p

    order = []
    for e in range(n):
        rem = sorted([k for k in range(ng) if k != gi[e]], key=lambda k: links(gi[e], k))
        if needy[e]:
            rem = needy[e] + [k for k in rem if k not in needy[e]]
        elif job[e] is not None:
            rem = [k for k in rem if k != job[e][1]] + [job[e][1]]
        order.append([gi[e]] + rem)

    hop2 = [[] for _ in range(n)]
    for k in range(ng):
        dests = [d for d in range(n) if gi[d] != k]
        elig = {d: [s for s in groups[k] if topo.may_write(cores[s], cores[d])] for d in dests}
        for d in sorted(dests, key=lambda d: len(elig[d])):
            s = min(elig[d], key=lambda s: len(hop2[s]))
            hop2[s].append(d)
    for s in range(n):
        hop2[s].sort(key=lambda d: (order[d].index(gi[s]), 0 if needy[d] else 1))

    lcol = [[None] * n for _ in range(n)]
    for r in range(n):
        for k in range(ng):
            B = k * _LG + _TOK
            nd = [e for e in groups[k] if gi[r] in needy[e]]
            if not nd:
                for j, e in enumerate(groups[k]):
                    lcol[r][e] = B + j * _TOK
            else:
                e = nd[0]
                p = via[(e, gi[r])]
                o = [x for x in groups[k] if x != e and x != p][0]
                first = groups[gi[r]].index(r) == 0
                lcol[r][p] = B if first else B + _TOK
                lcol[r][e] = B + _TOK if first else B
                lcol[r][o] = B + 2 * _TOK

    calls = [[] for _ in range(n)]
    expect = [[0] * ng for _ in range(n)]
    for e in range(n):
        E = eng[e]
        hf, qt = len(E) // 2, len(E) // 4
        pats = [[E[0:hf], E[hf:hf + qt], E[hf + qt:]], [E[hf:], E[0:qt], E[qt:hf]]]
        sl = "sl%d" % gi[e]
        for idx, k in enumerate(order[e]):
            if idx == 0:
                peers = [r for r in groups[k] if r != e]
                new = [([("sc%d" % k, 1)], [(r, "ro%d" % k, groups[k].index(r) * _TOK, _TOK, "land", lcol[r][e], sl, en)
                                            for r, en in zip(peers, [E[0:hf], E[hf:]])])]
            elif k in needy[e]:
                new = [([("sc%d" % k, 1)], [(via[(e, k)], "ro%d" % k, 0, _GW, "zz", _TOK, "sq", E)])]
            elif job[e] is not None and job[e][1] == k:
                ha, hb, hc = groups[k]
                pt = pats[idx - 1]
                new = [([("sc%d" % k, 1)], [(hb, "ro%d" % k, _TOK, _TOK, "land", lcol[hb][e], sl, E)]),
                       ([("sz", 2), ("sq", len(eng[job[e][0]]))],
                        [(ha, "zz", 0, 2 * _TOK, "land", lcol[ha][e], sl, pt[0]),
                         (hb, "zz", _TOK, 2 * _TOK, "land", lcol[hb][job[e][0]] - _TOK, sl, pt[1]),
                         (hc, "zz", 3 * _TOK, 2 * _TOK, "land", lcol[hc][job[e][0]], sl, pt[2])])]
            else:
                new = [([("sc%d" % k, 1)], [(r, "ro%d" % k, j * _TOK, _TOK, "land", lcol[r][e], sl, en)
                                            for j, (r, en) in enumerate(zip(groups[k], pats[idx - 1]))])]
            calls[e] += new
            for _w, tr in new:
                for t in tr:
                    if t[4] == "land":
                        expect[t[0]][gi[e]] += len(t[7])

    corder = []
    for r in range(n):
        rem = [k for k in range(ng) if k != gi[r]]
        rem.sort(key=lambda k: (1 if any(gi[r] in needy[p] for p in groups[k]) else 0, links(k, gi[r])))
        corder.append([gi[r]] + rem)
    ilv = [len(needy[e]) == ng - 1 for e in range(n)]
    return dict(cores=cores, groups=groups, gi=gi, eng=eng, ilv=ilv, needy=needy, job=job, order=order, hop2=hop2,
                lcol=lcol, calls=calls, expect=expect, corder=corder)


def rank_program(g, core, T, topo):
    me = T.rank_of(core)
    if me is None:
        return
    P = _plan(T, topo)
    S = T.sem
    cores, groups, gi = P["cores"], P["groups"], P["gi"]
    route = T.tables["ROUTE"]
    k0 = gi[me]
    E = P["eng"][me]
    order = P["order"][me]
    co = P["corder"][me]
    v, tq = g.vector, g.tensor
    own = me * _TOK
    loc = [0]

    def dst_id(r):
        rid, pid, _se = topo.addr(cores[r])
        return DstId(rid=rid, pnc=pid)

    g.sync.dma_start(T.xall[:, own:own + _TOK], T.x[:, :]).then_inc(S.sx, 16)
    g.scalar.dma_start(T.grow[0:1, 0:2 * _TOK], T.gate[:, :]).then_inc(S.sg, 16)
    g.scalar.dma_start(T.w1s[:, :], T.w1[:, :]).then_inc(S.sw1, 16)
    g.sync.dma_start(T.w2s[:, :], T.w2[:, :]).then_inc(S.sw2, 16)

    g.wait_ge(S.sx, 16)
    peers = [r for r in groups[k0] if r != me]
    blk = T.xall[:, own:own + _TOK]
    g.remote_dma_fused([RemoteDMATransfer(dst_ids=[dst_id(r) for r in peers], dma_engine_mask=_m(E),
                                          remote_sem=S["sxg%d" % k0], srcs=[blk], dsts=[blk for _ in peers])],
                       local_sem=S.sloc)
    loc[0] += len(E)
    if P["hop2"][me]:
        g.wait_ge(S["sxg%d" % k0], len(E) * len(peers))
        cb = T.xall[:, k0 * _GW:(k0 + 1) * _GW]
        g.remote_dma_fused([RemoteDMATransfer(dst_ids=[dst_id(d) for d in P["hop2"][me]], dma_engine_mask=_m(E),
                                              remote_sem=S["sxg%d" % k0], srcs=[cb], dsts=[cb for _ in P["hop2"][me]])],
                           local_sem=S.sloc)
        loc[0] += len(E)
    for waits, tr in P["calls"][me]:
        for sem, cnt in waits:
            g.wait_ge(S[sem], cnt)
        g.remote_dma_fused([RemoteDMATransfer(dst_ids=[dst_id(r)], dma_engine_mask=_m(en), remote_sem=S[rs],
                                              src=T[sb][:, sc:sc + w], dst=T[db][:, dc:dc + w])
                            for (r, sb, sc, w, db, dc, rs, en) in tr], local_sem=S.sloc)
        loc[0] += sum(len(t[7]) for t in tr)
    g.wait_ge(S.sloc, loc[0])

    runs = {k: [] for k in co}
    for i in range(len(route[me][0])):
        t = 0
        while t < _TOK:
            e = route[me][t][i]
            u = t + 1
            while u < _TOK and route[me][u][i] == e:
                u += 1
            runs[gi[e]].append((i * _TOK + t, P["lcol"][me][e] + t, u - t))
            t = u
    ngm = sum(len(r) for r in runs.values())

    def gm(k):
        for (gc, lc, ln) in runs[k]:
            tq.matmul(T.pm[:, lc:lc + ln], T.ones[0:1, :], T.grow[0:1, gc:gc + ln], True, True).then_inc(S.sgm, 1)

    def pa(idx, hf):
        return T["pa%d%d" % (idx % 2, hf)]

    HW = _HT * _GW

    def mm1(idx, k):
        if idx == 0:
            tq.wait_ge(S.sx, 16)
            tq.wait_ge(S.sw1, 16)
            tq.wait_ge(S["sxg%d" % k], len(E) * len(peers))
        else:
            tq.wait_ge(S["sxg%d" % k], len(E))
        for f in range(_FT):
            hf, q = f // _HT, f % _HT
            tq.matmul(pa(idx, hf)[:, q * _GW:(q + 1) * _GW], T.w1s[:, f * 128:(f + 1) * 128],
                      T.xall[:, k * _GW:(k + 1) * _GW], True, True).then_inc(S[("sab%d" if hf else "saa%d") % k], 1)

    def mm2(idx, k):
        if idx == 0:
            tq.wait_ge(S.sw2, 16)
        for f in range(_FT):
            if f % _HT == 0:
                tq.wait_ge(S[("shb%d" if f // _HT else "sha%d") % k], 1)
            tq.matmul(T["pr%d" % k][:, 0:_GW], T.w2s[:, f * 128:(f + 1) * 128],
                      T["h%d" % k][:, f * _GW:(f + 1) * _GW], f == 0, f == _FT - 1).then_inc(S["sr%d" % k], 1)

    tq.wait_ge(S.sone, 1)
    tq.wait_ge(S.sg, 16)
    tq.wait_ge(S.spm, 1)
    gm(co[0])
    gm(co[1])
    mm1(0, order[0])
    mm2(0, order[0])
    if P["ilv"][me]:
        mm1(1, order[1])
        mm1(2, order[2])
        mm2(1, order[1])
        mm2(2, order[2])
    else:
        mm1(1, order[1])
        mm2(1, order[1])
        mm1(2, order[2])
        mm2(2, order[2])
    gm(co[2])

    vc = [0]

    def vop(inst):
        inst.then_inc(S.sv, 1)
        vc[0] += 1

    def vsync():
        v.wait_ge(S.sv, vc[0])

    v.memset(T.ones[0:1, :], 1.0).then_inc(S.sone, 1)
    v.memset(T.pm[:, 0:_NG * _LG], 0.0).then_inc(S.spm, 1)
    vop(v.memset(T.zer[:, 0:HW], 0.0))
    vsync()
    job = P["job"][me]

    def relu(idx, k):
        for hf in range(2):
            v.wait_ge(S[("sab%d" if hf else "saa%d") % k], _HT)
            v.tensor_tensor(T["h%d" % k][:, hf * HW:(hf + 1) * HW], pa(idx, hf)[:, 0:HW], T.zer[:, 0:HW],
                            AluOpType.max).then_inc(S[("shb%d" if hf else "sha%d") % k], 1)

    def out(idx, k):
        v.wait_ge(S["sr%d" % k], _FT)
        if job is not None and job[1] == k:
            pr = T["pr%d" % k]
            v.tensor_copy(T["ro%d" % k][:, _TOK:2 * _TOK], pr[:, _TOK:2 * _TOK]).then_inc(S["sc%d" % k], 1)
            v.tensor_copy(T.zz[:, 0:_TOK], pr[:, 0:_TOK]).then_inc(S.sz, 1)
            v.tensor_copy(T.zz[:, 4 * _TOK:5 * _TOK], pr[:, 2 * _TOK:3 * _TOK]).then_inc(S.sz, 1)
        else:
            v.tensor_copy(T["ro%d" % k][:, :], T["pr%d" % k][:, 0:_GW]).then_inc(S["sc%d" % k], 1)
        if idx == 0:
            j = groups[k].index(me)
            c = P["lcol"][me][me]
            vop(v.tensor_copy(T.land[:, c:c + _TOK], T["pr%d" % k][:, j * _TOK:(j + 1) * _TOK]))

    relu(0, order[0])
    out(0, order[0])
    if P["ilv"][me]:
        relu(1, order[1])
        relu(2, order[2])
        out(1, order[1])
        out(2, order[2])
    else:
        relu(1, order[1])
        out(1, order[1])
        relu(2, order[2])
        out(2, order[2])
    v.wait_ge(S.sgm, ngm)
    acc = None
    for idx, k in enumerate(co):
        v.wait_ge(S["sl%d" % k], P["expect"][me][k])
        vsync()
        a, b = k * _LG + _TOK, (k + 1) * _LG
        vop(v.tensor_tensor(T.prod[:, a:b], T.land[:, a:b], T.pm[:, a:b], AluOpType.mult))
        vsync()
        t0 = T.tmp[:, (3 * idx) * _TOK:(3 * idx + 1) * _TOK]
        t1 = T.tmp[:, (3 * idx + 1) * _TOK:(3 * idx + 2) * _TOK]
        t2 = T.tmp[:, (3 * idx + 2) * _TOK:(3 * idx + 3) * _TOK]
        vop(v.tensor_tensor(t0, T.prod[:, a:a + _TOK], T.prod[:, a + _TOK:a + 2 * _TOK], AluOpType.add))
        third = T.prod[:, a + 2 * _TOK:b]
        if acc is not None:
            vop(v.tensor_tensor(t1, third, acc, AluOpType.add))
            third = t1
        vsync()
        if idx == len(co) - 1:
            v.tensor_tensor(T.ybf[:, :], t0, third, AluOpType.add).then_inc(S.syr, 1)
        else:
            vop(v.tensor_tensor(t2, t0, third, AluOpType.add))
            acc = t2

    g.sync.wait_ge(S.syr, 1)
    g.sync.dma_start(T.y[:, :], T.ybf[:, :]).then_inc(S.sy, 16)
    g.sync.wait_ge(S.sy, 16)
